import numpy as np
import ml_dtypes


def mxq(x, axis, fmt="e4m3"):
    dtype, down = {"e4m3": (ml_dtypes.float8_e4m3fn, 7), "e5m2": (ml_dtypes.float8_e5m2, 14)}[fmt]
    v = np.moveaxis(np.asarray(x, np.float32).astype(ml_dtypes.bfloat16).astype(np.float64), axis, -1)
    blocks = v.reshape(v.shape[:-1] + (-1, 32))
    amax = np.abs(blocks).max(-1, keepdims=True)
    byte = np.maximum(np.where(amax > 0, np.frexp(amax)[1] - 1 + 127, 0) - down, 1)
    scale = np.exp2(byte - 127.0)
    codes = (blocks / scale).astype(np.float32).astype(dtype).astype(np.float64)
    return np.moveaxis((codes * scale).reshape(v.shape), -1, axis)


WIDE = False


def mx_kscale(k):
    if not WIDE:
        return np.ones(k)
    levels = np.array([10, -10, 5, -5, 0])
    if k % 512:
        return np.exp2(np.random.permutation(np.resize(levels, k // 32))).repeat(32)
    a = np.empty((k // 512, 16))
    for p in range(k // 512):
        a[p, :8] = np.random.permutation(np.resize(levels, 8))
        for g in range(8):
            far = levels[np.abs(levels - a[p, g]) >= 10]
            a[p, g + 8] = far[np.random.randint(len(far))]
    return np.exp2(a.ravel()).repeat(32)


BF16 = ml_dtypes.bfloat16


def bf(x):
    return np.asarray(x, np.float32).astype(BF16)


def f64(x):
    return np.asarray(x).astype(np.float64)

def planes(Y):
    n, m = Y.shape
    b = f64(bf(Y)).reshape(n // 32, 32, m)
    amax = np.abs(b).max(1)
    byte = np.clip(np.where(amax > 0, np.frexp(amax)[1] - 1 + 127 - 7, 1), 1, 254)
    codes = (b * np.exp2(127.0 - byte)[:, None, :]).reshape(n, m).astype(np.float32).astype(ml_dtypes.float8_e4m3fn).view(np.uint8)
    words = codes.reshape(n // 512, 128, 4, m).transpose(0, 1, 3, 2)
    return np.ascontiguousarray(words), np.ascontiguousarray(byte.astype(np.uint8).reshape(n // 512, 16, m))


S, P, E, H, V, D = 1024, 4, 256, 1024, 4096, 512


def setup_inputs():
    s1 = mx_kscale(P * E)
    s2 = mx_kscale(V)
    t = mx_kscale(S)
    spread = np.exp(0.8 * np.random.randn(H))
    prev = np.random.randn(S, P * E) * s1
    context = np.random.randn(P * E, H) / np.sqrt(P * E) / s1[:, None]
    sample_weight = np.exp(0.3 * np.random.randn(S)) * t
    err = 0.3 * np.random.randn(S, V) * s2 / t[:, None]
    vocab = np.random.randn(V, D) / np.sqrt(V) / s2[:, None]
    bottleneck = 0.5 * spread[:, None] * np.random.randn(H, D)
    rate = 0.15 * spread
    return {"prev": bf(prev), "context": bf(context), "sample_weight": bf(sample_weight),
            "err": bf(err), "vocab": bf(vocab), "bottleneck": bf(bottleneck), "rate": bf(rate)}


def reference(prev, context, sample_weight, err, vocab, bottleneck, rate):
    pre = mxq(f64(prev), 1, "e4m3") @ mxq(f64(context), 0, "e4m3")
    hidden = np.tanh(pre) * f64(sample_weight)[:, None]
    back = mxq(f64(err), 1, "e4m3") @ mxq(f64(vocab), 0, "e4m3")
    grad = mxq(hidden, 0, "e4m3").T @ mxq(back, 0, "e4m3")
    y = f64(bottleneck) - f64(rate)[:, None] * grad
    words, scales = planes(y)
    return y, words, scales

@@ -1,0 +1,392 @@
+from contextlib import ExitStack
+
+import concourse.mybir as mybir
+from concourse.masks import make_identity
+
+S, F, H, V, D = 1024, 1024, 1024, 4096, 512
+FLOPS = 2 * S * F * H + 2 * S * V * D + 2 * S * H * D
+
+F32 = mybir.dt.float32
+BF16 = mybir.dt.bfloat16
+U32 = mybir.dt.uint32
+I32 = mybir.dt.int32
+U8 = mybir.dt.uint8
+FP8X4 = mybir.dt.float8_e4m3fn_x4
+ALU = mybir.AluOpType
+ACT = mybir.ActivationFunctionType
+
+P = 128
+PACK = 4
+KP = P * PACK
+VS = 256
+A0 = 192
+
+
+def tile_output_bottleneck_update_h3_kernel(
+    tc, prev, context, sample_weight, err, vocab, bottleneck, rate, out_0, out_1, out_2
+):
+    nc = tc.nc
+    with ExitStack() as ctx:
+        keep = ctx.enter_context(tc.tile_pool(name="keep", bufs=1))
+        stage = ctx.enter_context(tc.tile_pool(name="stage", bufs=2))
+        tps = ctx.enter_context(tc.psum_pool(name="tps", bufs=4))
+        aps = ctx.enter_context(tc.psum_pool(name="aps", bufs=4))
+        ctx.enter_context(tc.manual_schedule())
+
+        def mx_tiles(pool, name, width, bufs=None):
+            codes = pool.tile([P, width], U32, name=name + "_codes", bufs=bufs, align_bytes=64)
+            scales = pool.tile([P, width], U8, name=name + "_scales", bufs=bufs, align_bytes=64)
+            return codes, scales
+
+        def load(name, shape, src, bufs):
+            t = stage.tile(shape, BF16, name=name, bufs=bufs, align_bytes=64)
+            nc.sync.dma_start(out=t[:], in_=src)
+            return t
+
+        def copy_on(engine, out, in_):
+            if engine == "vector":
+                nc.vector.tensor_copy(out=out, in_=in_)
+            else:
+                nc.scalar.copy(out=out, in_=in_)
+
+        def interleave(engine, grouped, rows, c0, c1, run=4):
+            copy_on(
+                engine,
+                grouped[:, c0:c1, :].rearrange("p (c i) t -> p c t i", i=run),
+                rows[:, :, c0:c1].rearrange("p t (c i) -> p c t i", i=run),
+            )
+
+        def quantize(mx, c0, grouped_flat):
+            n = grouped_flat.shape[1] // PACK
+            nc.vector.quantize_mx(
+                out=mx[0][:, c0 : c0 + n].bitcast(FP8X4), scales=mx[1][:, c0 : c0 + n], in_=grouped_flat
+            )
+
+        def mm(out, lhs, l0, rhs, r0, n, start, stop):
+            nc.tensor.matmul_mx(
+                out=out,
+                lhsT=lhs[0][:, l0 : l0 + P].bitcast(FP8X4),
+                lhsT_scale=lhs[1][:, l0 : l0 + P],
+                rhs=rhs[0][:, r0 : r0 + n].bitcast(FP8X4),
+                rhs_scale=rhs[1][:, r0 : r0 + n],
+                start=start,
+                stop=stop,
+            )
+
+        def transpose_unit(rows):
+            words = rows.bitcast(F32)
+            bank = tps.tile([P, 2, 2, P], F32, name="tbank")
+            for g in range(2):
+                for u in range(2):
+                    nc.tensor.transpose(bank[:, g, u, :], words[:, 256 * g + u : 256 * (g + 1) : 2], ident[:])
+            return bank
+
+        def empty_unit(engine, bank, grouped, j):
+            dst = grouped[:, 1024 * j : 1024 * (j + 1)].bitcast(F32).rearrange("p (g r u) -> p g r u", g=2, u=2)
+            copy_on(engine, dst, bank[:].rearrange("p g u r -> p g r u"))
+
+        def turn(sources, engines):
+            halves = []
+            for h in range(2):
+                grouped = stage.tile([P, 2048], BF16, name="turned", bufs=4, align_bytes=64)
+                for j in range(2):
+                    bank = transpose_unit(sources[2 * h + j])
+                    empty_unit(engines[2 * h + j], bank, grouped, j)
+                halves.append(grouped)
+            return halves
+
+        def quantize_turned(halves):
+            res = []
+            for h in range(2):
+                mx = mx_tiles(stage, "tq", 512, 10)
+                quantize(mx, 0, halves[h][:])
+                res.append(mx)
+            return res
+
+        ident = keep.tile([P, P], F32, name="ident")
+        make_identity(nc, ident[:])
+        warm = keep.tile([P, 1], F32, name="warm")
+        nc.scalar.activation(out=warm[:], in_=ident[:, 0:1], func=ACT.Tanh)
+
+        def slots(x, g):
+            return x[KP * g : KP * (g + 1), :].rearrange("(p t) c -> p t c", t=PACK)
+
+        def load_k(src):
+            return load("krows", [P, PACK, 512], src, 7)
+
+        def load_s(shape, src):
+            return load("srows", shape, src, 4)
+
+        def flat(grouped):
+            return grouped[:].rearrange("p c t -> p (c t)")
+
+        def new_grouped(width=512):
+            grouped = stage.tile([P, width, PACK], BF16, name="grouped", bufs=4, align_bytes=64)
+            return grouped
+
+        vq = [mx_tiles(keep, "vq%d" % k, D) for k in range(8)]
+        cq = [[mx_tiles(keep, "cq%d%d" % (k, g), 512) for g in range(2)] for k in range(2)]
+        hq = [[mx_tiles(keep, "hq%d%d" % (s, g), 512) for g in range(2)] for s in range(2)]
+        bq0 = mx_tiles(keep, "bq0", D)
+        bq1 = [mx_tiles(keep, "bq1%d" % d, 256) for d in range(2)]
+        SC4 = ["scalar"] * 4
+
+        def regroup(src, mx, share):
+            width = src.shape[2]
+            grouped = new_grouped(width)
+            if share:
+                interleave("scalar", grouped, src, 0, share)
+            if share < width:
+                interleave("vector", grouped, src, share, width)
+            return lambda: quantize(mx, 0, flat(grouped))
+
+        def pre_pass(accs, pq, k, g):
+            for t in range(4):
+                mm(accs[t][:], pq[t // 2], 256 * (t % 2) + P * k, cq[k][g], 0, 512, k == 0, k == 1)
+
+        def tanh_out(th, t, acc):
+            nc.scalar.activation(
+                out=th[:, t, :].rearrange("p (j m) -> p j m", j=PACK),
+                in_=acc[:].rearrange("p (m j) -> p j m", j=PACK),
+                func=ACT.Tanh,
+            )
+
+        def new_th():
+            th = stage.tile([P, PACK, 512], F32, name="th", bufs=4, align_bytes=64)
+            return th
+
+        def new_acc(n=512):
+            acc = aps.tile([P, n], F32, name="acc")
+            return acc
+
+        def pre_block(g, pq):
+            th = new_th()
+            for t in range(4):
+                acc = new_acc()
+                for k in range(2):
+                    mm(acc[:], pq[t // 2], 256 * (t % 2) + P * k, cq[k][g], 0, 512, k == 0, k == 1)
+                tanh_out(th, t, acc)
+            return th
+
+        def weigh(s, g, th):
+            grouped = new_grouped()
+            nc.vector.tensor_tensor(
+                out=grouped[:].rearrange("p (c i) t -> p c t i", i=2),
+                in0=th[:].rearrange("p t (c i) -> p c t i", i=2),
+                in1=w32[:, s, :].unsqueeze(1).unsqueeze(3).to_broadcast([P, 256, PACK, 2]),
+                op=ALU.mult,
+            )
+            return lambda: quantize(hq[s][g], 0, flat(grouped))
+
+        craw = {}
+        e0, vraw, e1, braw = {}, {}, {}, {}
+
+        def load_c(k, g):
+            craw[k, g] = load_k(slots(context, k)[:, :, 512 * g : 512 * (g + 1)])
+
+        def load_v(k):
+            vraw[k] = load_k(slots(vocab, k))
+
+        def load_e0(c):
+            e0[c] = load_s([P, PACK, 1024], slots(err, 0)[:, :, 1024 * c : 1024 * (c + 1)])
+
+        def load_e1(t):
+            e1[t] = load_s([P, V], slots(err, 1)[:, t, :])
+
+        load_c(0, 0)
+        p0 = [load("p0", [P, F], slots(prev, 0)[:, t, :], 4) for t in range(4)]
+        load_c(1, 0)
+        p1 = load_s([P, PACK, F], slots(prev, 1))
+        load_e0(0)
+        load_c(0, 1)
+        load_c(1, 1)
+        load_v(0)
+        load_e0(1)
+        load_v(1)
+        w_raw = load("w_raw", [P, 2, PACK], sample_weight.rearrange("(g p t) -> p g t", g=2, t=PACK), 1)
+        r_raw = load("r_raw", [P, 2, PACK], rate.rearrange("(g p t) -> p g t", g=2, t=PACK), 1)
+        load_v(2)
+
+        q = regroup(craw[0, 0], cq[0][0], 0)
+        hp = turn([p0[t][:] for t in range(4)], SC4)
+        q()
+        pq0 = quantize_turned(hp)
+        q = regroup(craw[1, 0], cq[1][0], A0)
+        q()
+        load_v(3)
+        load_e0(2)
+        accs = [new_acc() for t in range(4)]
+        pre_pass(accs, pq0, 0, 0)
+        pre_pass(accs, pq0, 1, 0)
+        th = {}
+        th[0, 0] = new_th()
+        for t in range(4):
+            tanh_out(th[0, 0], t, accs[t])
+        hp = turn([p1[:, t, :] for t in range(4)], SC4)
+        q0 = regroup(craw[0, 1], cq[0][1], 0)
+        pq1 = quantize_turned(hp)
+        q1 = regroup(craw[1, 1], cq[1][1], 0)
+        q0()
+        q1()
+        load_v(4)
+        load_v(5)
+        load_e0(3)
+        halves = turn([e0[0][:, t, :] for t in range(4)], SC4)
+        th[1, 0] = pre_block(0, pq1)
+        th[0, 1] = pre_block(1, pq0)
+        eq = {0: quantize_turned(halves)}
+        qa = regroup(vraw[0], vq[0], 0)
+        qb = regroup(vraw[1], vq[1], 0)
+        qa()
+        qb()
+        load_v(6)
+        load_v(7)
+        load_e1(0)
+        w32 = keep.tile([P, 2, PACK], F32, name="w32")
+        nc.vector.tensor_copy(out=w32[:], in_=w_raw[:])
+        neg_rate = keep.tile([P, 2, PACK], F32, name="neg_rate")
+        nc.vector.tensor_scalar(out=neg_rate[:], in0=r_raw[:], scalar1=-1.0, scalar2=None, op0=ALU.mult)
+        halves = turn([e0[1][:, t, :] for t in range(4)], SC4)
+        th[1, 1] = pre_block(1, pq1)
+        qa = regroup(vraw[2], vq[2], 0)
+        eq[1] = quantize_turned(halves)
+        qb = regroup(vraw[3], vq[3], 0)
+        qa()
+        qb()
+        load_e1(1)
+
+        acc0 = [new_acc() for t in range(4)]
+
+        def back0_passes(c):
+            for t in range(4):
+                for g in range(2):
+                    mm(acc0[t][:], eq[c][t // 2], 256 * (t % 2) + P * g, vq[2 * c + g], 0, D, c == 0 and g == 0, c == 3 and g == 1)
+
+        def err1_turn(t):
+            return turn([e1[t][:, 1024 * j : 1024 * (j + 1)] for j in range(4)], SC4)
+
+        fq = {}
+        hs = [(0, 0), (1, 0), (0, 1), (1, 1)]
+        for c in range(2, 4):
+            qa = regroup(vraw[2 * c], vq[2 * c], 0)
+            back0_passes(c - 2)
+            halves = turn([e0[c][:, t, :] for t in range(4)], SC4)
+            load_e1(c)
+            qb = regroup(vraw[2 * c + 1], vq[2 * c + 1], VS)
+            qa()
+            q = weigh(*hs[c - 2], th[hs[c - 2]])
+            eq[c] = quantize_turned(halves)
+            qb()
+            q()
+        for g in range(2):
+            braw[g] = load_k(slots(bottleneck, g))
+        back0_passes(2)
+        halves = err1_turn(0)
+        q = weigh(*hs[2], th[hs[2]])
+        fq[0] = quantize_turned(halves)
+        q()
+        back0_passes(3)
+        rows0 = stage.tile([P, PACK, D], BF16, name="rows0", bufs=1, align_bytes=64)
+        for t in range(2):
+            nc.scalar.copy(out=rows0[:, t, :], in_=acc0[t][:])
+        halves = err1_turn(1)
+        for t in range(2, 4):
+            nc.vector.tensor_copy(out=rows0[:, t, :], in_=acc0[t][:])
+        q = weigh(*hs[3], th[hs[3]])
+        fq[1] = quantize_turned(halves)
+        q()
+        rows1 = [stage.tile([P, PACK, 256], BF16, name="rows1", bufs=2, align_bytes=64) for d in range(2)]
+
+        def back1(t, d):
+            acc = new_acc(256)
+            for k in range(8):
+                mm(acc[:], fq[t][k // 4], P * (k % 4), vq[k], 256 * d, 256, k == 0, k == 7)
+            nc.scalar.copy(out=rows1[d][:, t, :], in_=acc[:])
+
+        back1(0, 0)
+        halves = err1_turn(2)
+        q = regroup(rows0, bq0, 0)
+        fq[2] = quantize_turned(halves)
+        q()
+        back1(1, 0)
+        halves = err1_turn(3)
+        fq[3] = quantize_turned(halves)
+        back1(2, 0)
+        back1(0, 1)
+        back1(3, 0)
+        q = regroup(rows1[0], bq1[0], 0)
+        q()
+        back1(1, 1)
+        back1(2, 1)
+
+        ys = [[new_th() for g in range(2)] for d in range(2)]
+        yq = [mx_tiles(keep, "yq%d" % g, D) for g in range(2)]
+
+        def grad_pass(acc, g, t, d, s):
+            if s == 0:
+                mm(acc, hq[0][g], P * t, bq0, 256 * d, 256, True, False)
+            else:
+                mm(acc, hq[1][g], P * t, bq1[d], 0, 256, False, True)
+
+        def update(acc, g, t, d):
+            y = ys[d][g]
+            nc.vector.scalar_tensor_tensor(
+                out=y[:, t, 0:256], in0=acc, scalar=neg_rate[:, g, t : t + 1], in1=braw[g][:, t, 256 * d : 256 * (d + 1)],
+                op0=ALU.mult, op1=ALU.add,
+            )
+            if t == 3:
+                nc.sync.dma_start(out=slots(out_0, g)[:, :, 256 * d : 256 * (d + 1)], in_=y[:, :, 0:256])
+
+        def planes(g, d, share):
+            grouped = new_grouped(256)
+            interleave("scalar", grouped, ys[d][g], 0, share, 2)
+            if share < 256:
+                interleave("vector", grouped, ys[d][g], share, 256, 2)
+
+            def finish():
+                quantize(yq[g], 256 * d, flat(grouped))
+                cols = slice(256 * d, 256 * (d + 1))
+                nc.sync.dma_start(
+                    out=out_1[g, :, cols, :].rearrange("p m t -> p (m t)").bitcast(I32), in_=yq[g][0][:, cols].bitcast(I32)
+                )
+                if d == 1:
+                    for q4 in range(4):
+                        nc.sync.dma_start(
+                            out=out_2[g, 4 * q4 : 4 * q4 + 4, :].bitcast(I32),
+                            in_=yq[g][1][32 * q4 : 32 * q4 + 4, :].bitcast(I32),
+                        )
+
+            return finish
+
+        fin = []
+        for g in range(2):
+            for tp in range(2):
+                bank = tps.tile([P, 2, 256], F32, name="tbank")
+                for i in range(2):
+                    grad_pass(bank[:, i, :], g, 2 * tp + i, 0, 0)
+                    grad_pass(bank[:, i, :], g, 2 * tp + i, 0, 1)
+                for i in range(2):
+                    update(bank[:, i, :], g, 2 * tp + i, 0)
+            if g == 1:
+                back1(3, 1)
+            fin.append(planes(g, 0, 256))
+        q = regroup(rows1[1], bq1[1], 0)
+        fin[0]()
+        q()
+        gacc = {}
+        for g in range(2):
+            for t in range(4):
+                if g == 0:
+                    gacc[g, t] = new_acc(256)
+                else:
+                    gacc[g, t] = tps.tile([P, 256], F32, name="tbank")
+                grad_pass(gacc[g, t][:], g, t, 1, 0)
+        fin[1]()
+        fin = []
+        for g in range(2):
+            for t in range(4):
+                grad_pass(gacc[g, t][:], g, t, 1, 1)
+                update(gacc[g, t][:], g, t, 1)
+            fin.append(planes(g, 1, 256 if g == 0 else 96))
+        fin[0]()
+        fin[1]()

@@ -18,8 +18,13 @@ ACT = mybir.ActivationFunctionType
 P = 128
 PACK = 4
 KP = P * PACK
-VS = 256
-A0 = 192
+A0 = 160
+A1 = 192
+S3 = 256
+S5 = 512
+S7 = 512
+R0 = 0
+PIECES = [(0, 256), (256, 256)]
 
 
 def tile_output_bottleneck_update_h3_kernel(
@@ -73,24 +78,25 @@ def tile_output_bottleneck_update_h3_kernel(
                 stop=stop,
             )
 
-        def transpose_unit(rows):
+        def transpose_unit(rows, ready):
             words = rows.bitcast(F32)
             bank = tps.tile([P, 2, 2, P], F32, name="tbank")
             for g in range(2):
                 for u in range(2):
-                    nc.tensor.transpose(bank[:, g, u, :], words[:, 256 * g + u : 256 * (g + 1) : 2], ident[:])
+                    src = words[:, 256 * g + P * u : 256 * g + P * (u + 1)] if ready else words[:, 256 * g + u : 256 * (g + 1) : 2]
+                    nc.tensor.transpose(bank[:, g, u, :], src, ident[:])
             return bank
 
         def empty_unit(engine, bank, grouped, j):
             dst = grouped[:, 1024 * j : 1024 * (j + 1)].bitcast(F32).rearrange("p (g r u) -> p g r u", g=2, u=2)
             copy_on(engine, dst, bank[:].rearrange("p g u r -> p g r u"))
 
-        def turn(sources, engines):
+        def turn(sources, engines, ready=False):
             halves = []
             for h in range(2):
                 grouped = stage.tile([P, 2048], BF16, name="turned", bufs=4, align_bytes=64)
                 for j in range(2):
-                    bank = transpose_unit(sources[2 * h + j])
+                    bank = transpose_unit(sources[2 * h + j], ready)
                     empty_unit(engines[2 * h + j], bank, grouped, j)
                 halves.append(grouped)
             return halves
@@ -128,7 +134,7 @@ def tile_output_bottleneck_update_h3_kernel(
         cq = [[mx_tiles(keep, "cq%d%d" % (k, g), 512) for g in range(2)] for k in range(2)]
         hq = [[mx_tiles(keep, "hq%d%d" % (s, g), 512) for g in range(2)] for s in range(2)]
         bq0 = mx_tiles(keep, "bq0", D)
-        bq1 = [mx_tiles(keep, "bq1%d" % d, 256) for d in range(2)]
+        bq1 = [mx_tiles(keep, "bq1%d" % d0, w) for d0, w in PIECES]
         SC4 = ["scalar"] * 4
 
         def regroup(src, mx, share):
@@ -193,67 +199,67 @@ def tile_output_bottleneck_update_h3_kernel(
         def load_e1(t):
             e1[t] = load_s([P, V], slots(err, 1)[:, t, :])
 
-        load_c(0, 0)
+        def turn_e0(c):
+            return turn([e0[c][:, t, :] for t in range(4)], SC4)
+
+        def turn_e1(t):
+            return turn([e1[t][:, 1024 * j : 1024 * (j + 1)] for j in range(4)], SC4)
+
         p0 = [load("p0", [P, F], slots(prev, 0)[:, t, :], 4) for t in range(4)]
-        load_c(1, 0)
+        load_c(0, 0)
         p1 = load_s([P, PACK, F], slots(prev, 1))
+        load_c(1, 0)
         load_e0(0)
         load_c(0, 1)
         load_c(1, 1)
-        load_v(0)
         load_e0(1)
+        load_v(0)
         load_v(1)
+        load_v(2)
         w_raw = load("w_raw", [P, 2, PACK], sample_weight.rearrange("(g p t) -> p g t", g=2, t=PACK), 1)
         r_raw = load("r_raw", [P, 2, PACK], rate.rearrange("(g p t) -> p g t", g=2, t=PACK), 1)
-        load_v(2)
 
-        q = regroup(craw[0, 0], cq[0][0], 0)
         hp = turn([p0[t][:] for t in range(4)], SC4)
-        q()
-        pq0 = quantize_turned(hp)
-        q = regroup(craw[1, 0], cq[1][0], A0)
-        q()
+        pq0 = [mx_tiles(stage, "tq", 512, 10) for h in range(2)]
+        quantize(pq0[0], 0, hp[0][:])
+        q0 = regroup(craw[0, 0], cq[0][0], A0)
+        quantize(pq0[1], 0, hp[1][:])
+        q0()
         load_v(3)
-        load_e0(2)
         accs = [new_acc() for t in range(4)]
         pre_pass(accs, pq0, 0, 0)
+        regroup(craw[1, 0], cq[1][0], A1)()
+        hp = turn([p1[:, t, :] for t in range(4)], ["scalar", "vector", "vector", "vector"])
+        load_e0(2)
+        load_v(4)
         pre_pass(accs, pq0, 1, 0)
         th = {}
         th[0, 0] = new_th()
         for t in range(4):
             tanh_out(th[0, 0], t, accs[t])
-        hp = turn([p1[:, t, :] for t in range(4)], SC4)
-        q0 = regroup(craw[0, 1], cq[0][1], 0)
         pq1 = quantize_turned(hp)
+        halves = turn_e0(0)
+        q0 = regroup(craw[0, 1], cq[0][1], 0)
         q1 = regroup(craw[1, 1], cq[1][1], 0)
         q0()
         q1()
-        load_v(4)
+        eq = {0: quantize_turned(halves)}
         load_v(5)
         load_e0(3)
-        halves = turn([e0[0][:, t, :] for t in range(4)], SC4)
+        load_v(6)
         th[1, 0] = pre_block(0, pq1)
-        th[0, 1] = pre_block(1, pq0)
-        eq = {0: quantize_turned(halves)}
+        halves = turn_e0(1)
         qa = regroup(vraw[0], vq[0], 0)
         qb = regroup(vraw[1], vq[1], 0)
         qa()
         qb()
-        load_v(6)
+        eq[1] = quantize_turned(halves)
         load_v(7)
         load_e1(0)
-        w32 = keep.tile([P, 2, PACK], F32, name="w32")
-        nc.vector.tensor_copy(out=w32[:], in_=w_raw[:])
-        neg_rate = keep.tile([P, 2, PACK], F32, name="neg_rate")
-        nc.vector.tensor_scalar(out=neg_rate[:], in0=r_raw[:], scalar1=-1.0, scalar2=None, op0=ALU.mult)
-        halves = turn([e0[1][:, t, :] for t in range(4)], SC4)
+        th[0, 1] = pre_block(1, pq0)
         th[1, 1] = pre_block(1, pq1)
-        qa = regroup(vraw[2], vq[2], 0)
-        eq[1] = quantize_turned(halves)
-        qb = regroup(vraw[3], vq[3], 0)
-        qa()
-        qb()
-        load_e1(1)
+        w32 = keep.tile([P, 2, PACK], F32, name="w32")
+        neg_rate = keep.tile([P, 2, PACK], F32, name="neg_rate")
 
         acc0 = [new_acc() for t in range(4)]
 
@@ -262,131 +268,174 @@ def tile_output_bottleneck_update_h3_kernel(
                 for g in range(2):
                     mm(acc0[t][:], eq[c][t // 2], 256 * (t % 2) + P * g, vq[2 * c + g], 0, D, c == 0 and g == 0, c == 3 and g == 1)
 
-        def err1_turn(t):
-            return turn([e1[t][:, 1024 * j : 1024 * (j + 1)] for j in range(4)], SC4)
-
         fq = {}
-        hs = [(0, 0), (1, 0), (0, 1), (1, 1)]
-        for c in range(2, 4):
-            qa = regroup(vraw[2 * c], vq[2 * c], 0)
-            back0_passes(c - 2)
-            halves = turn([e0[c][:, t, :] for t in range(4)], SC4)
-            load_e1(c)
-            qb = regroup(vraw[2 * c + 1], vq[2 * c + 1], VS)
-            qa()
-            q = weigh(*hs[c - 2], th[hs[c - 2]])
-            eq[c] = quantize_turned(halves)
-            qb()
-            q()
+        qa = regroup(vraw[2], vq[2], 0)
+        qb = regroup(vraw[3], vq[3], S3)
+        nc.vector.tensor_copy(out=w32[:], in_=w_raw[:])
+        nc.vector.tensor_scalar(out=neg_rate[:], in0=r_raw[:], scalar1=-1.0, scalar2=None, op0=ALU.mult)
+        qa()
+        back0_passes(0)
+        halves = turn_e0(2)
+        load_e1(1)
+        qa = regroup(vraw[4], vq[4], 0)
+        qb()
+        qa()
+        qb = regroup(vraw[5], vq[5], S5)
+        eq[2] = quantize_turned(halves)
+        back0_passes(1)
+        halves = turn_e0(3)
+        load_e1(2)
+        qa = regroup(vraw[6], vq[6], 0)
+        qb()
+        qa()
+        qb = regroup(vraw[7], vq[7], S7)
+        qh = weigh(0, 0, th[0, 0])
+        eq[3] = quantize_turned(halves)
+        qb()
+        qh()
+        back0_passes(2)
+        halves = turn_e1(0)
+        load_e1(3)
         for g in range(2):
             braw[g] = load_k(slots(bottleneck, g))
-        back0_passes(2)
-        halves = err1_turn(0)
-        q = weigh(*hs[2], th[hs[2]])
+        qh = weigh(1, 0, th[1, 0])
         fq[0] = quantize_turned(halves)
-        q()
+        qh()
         back0_passes(3)
         rows0 = stage.tile([P, PACK, D], BF16, name="rows0", bufs=1, align_bytes=64)
-        for t in range(2):
+        for t in range(0, 2):
             nc.scalar.copy(out=rows0[:, t, :], in_=acc0[t][:])
-        halves = err1_turn(1)
+        halves = turn_e1(1)
         for t in range(2, 4):
-            nc.vector.tensor_copy(out=rows0[:, t, :], in_=acc0[t][:])
-        q = weigh(*hs[3], th[hs[3]])
+            nc.scalar.copy(out=rows0[:, t, :], in_=acc0[t][:])
+        qh = weigh(0, 1, th[0, 1])
         fq[1] = quantize_turned(halves)
-        q()
-        rows1 = [stage.tile([P, PACK, 256], BF16, name="rows1", bufs=2, align_bytes=64) for d in range(2)]
+        qh()
+        acc1 = [aps.tile([P, PACK, P], F32, name="acc") for j in range(4)]
 
-        def back1(t, d):
-            acc = new_acc(256)
-            for k in range(8):
-                mm(acc[:], fq[t][k // 4], P * (k % 4), vq[k], 256 * d, 256, k == 0, k == 7)
-            nc.scalar.copy(out=rows1[d][:, t, :], in_=acc[:])
+        def back1(t, quarters):
+            for j in quarters:
+                for k in range(8):
+                    mm(acc1[j][:, t, :], fq[t][k // 4], P * (k % 4), vq[k], P * j, P, k == 0, k == 7)
 
-        back1(0, 0)
-        halves = err1_turn(2)
-        q = regroup(rows0, bq0, 0)
+        def back1_out(j):
+            grouped = new_grouped(P)
+            nc.scalar.copy(out=grouped[:], in_=acc1[j][:].rearrange("p t d -> p d t"))
+            return lambda: quantize(bq1[j // 2], P * (j % 2), flat(grouped))
+
+        back1(0, [0, 1])
+        halves = turn_e1(2)
+        qh = weigh(1, 1, th[1, 1])
         fq[2] = quantize_turned(halves)
-        q()
-        back1(1, 0)
-        halves = err1_turn(3)
+        qh()
+        back1(0, [2, 3])
+        back1(1, [0, 1])
+        halves = turn_e1(3)
+        qb = regroup(rows0, bq0, R0)
         fq[3] = quantize_turned(halves)
-        back1(2, 0)
-        back1(0, 1)
-        back1(3, 0)
-        q = regroup(rows1[0], bq1[0], 0)
-        q()
-        back1(1, 1)
-        back1(2, 1)
+        qb()
+        back1(2, [0, 1])
+        back1(1, [2, 3])
+        for j in range(2):
+            back1(3, [j])
+            back1_out(j)()
+        back1(2, [2, 3])
 
-        ys = [[new_th() for g in range(2)] for d in range(2)]
-        yq = [mx_tiles(keep, "yq%d" % g, D) for g in range(2)]
+        ys = {}
+        yq = mx_tiles(keep, "yq", 2 * D)
 
         def grad_pass(acc, g, t, d, s):
+            d0, w = PIECES[d]
             if s == 0:
-                mm(acc, hq[0][g], P * t, bq0, 256 * d, 256, True, False)
+                mm(acc, hq[0][g], P * t, bq0, d0, w, True, False)
             else:
-                mm(acc, hq[1][g], P * t, bq1[d], 0, 256, False, True)
+                mm(acc, hq[1][g], P * t, bq1[d], 0, w, False, True)
 
         def update(acc, g, t, d):
-            y = ys[d][g]
+            d0, w = PIECES[d]
+            if t == 0:
+                ys[d, g] = new_th()
+            y = ys[d, g]
             nc.vector.scalar_tensor_tensor(
-                out=y[:, t, 0:256], in0=acc, scalar=neg_rate[:, g, t : t + 1], in1=braw[g][:, t, 256 * d : 256 * (d + 1)],
+                out=y[:, t, 0:w], in0=acc, scalar=neg_rate[:, g, t : t + 1], in1=braw[g][:, t, d0 : d0 + w],
                 op0=ALU.mult, op1=ALU.add,
             )
-            if t == 3:
-                nc.sync.dma_start(out=slots(out_0, g)[:, :, 256 * d : 256 * (d + 1)], in_=y[:, :, 0:256])
+            if t % 2:
+                nc.sync.dma_start(out=slots(out_0, g)[:, t - 1 : t + 1, d0 : d0 + w], in_=y[:, t - 1 : t + 1, 0:w])
 
         def planes(g, d, share):
-            grouped = new_grouped(256)
-            interleave("scalar", grouped, ys[d][g], 0, share, 2)
-            if share < 256:
-                interleave("vector", grouped, ys[d][g], share, 256, 2)
+            d0, w = PIECES[d]
+            grouped = new_grouped(w)
+            interleave("scalar", grouped, ys[d, g], 0, share, 2)
+            if share < w:
+                interleave("vector", grouped, ys[d, g], share, w, 2)
 
             def finish():
-                quantize(yq[g], 256 * d, flat(grouped))
-                cols = slice(256 * d, 256 * (d + 1))
+                quantize(yq, D * g + d0, flat(grouped))
+                cols = slice(d0, d0 + w)
                 nc.sync.dma_start(
-                    out=out_1[g, :, cols, :].rearrange("p m t -> p (m t)").bitcast(I32), in_=yq[g][0][:, cols].bitcast(I32)
+                    out=out_1[g, :, cols, :].rearrange("p m t -> p (m t)").bitcast(I32), in_=yq[0][:, D * g + d0 : D * g + d0 + w].bitcast(I32)
                 )
-                if d == 1:
-                    for q4 in range(4):
-                        nc.sync.dma_start(
-                            out=out_2[g, 4 * q4 : 4 * q4 + 4, :].bitcast(I32),
-                            in_=yq[g][1][32 * q4 : 32 * q4 + 4, :].bitcast(I32),
-                        )
 
             return finish
 
-        fin = []
-        for g in range(2):
+        def grad_closed(g, d, share):
+            d0, w = PIECES[d]
             for tp in range(2):
-                bank = tps.tile([P, 2, 256], F32, name="tbank")
+                bank = tps.tile([P, 2, w], F32, name="tbank")
                 for i in range(2):
-                    grad_pass(bank[:, i, :], g, 2 * tp + i, 0, 0)
-                    grad_pass(bank[:, i, :], g, 2 * tp + i, 0, 1)
+                    grad_pass(bank[:, i, :], g, 2 * tp + i, d, 0)
+                    grad_pass(bank[:, i, :], g, 2 * tp + i, d, 1)
                 for i in range(2):
-                    update(bank[:, i, :], g, 2 * tp + i, 0)
-            if g == 1:
-                back1(3, 1)
-            fin.append(planes(g, 0, 256))
-        q = regroup(rows1[1], bq1[1], 0)
-        fin[0]()
-        q()
-        gacc = {}
-        for g in range(2):
+                    update(bank[:, i, :], g, 2 * tp + i, d)
+            return planes(g, d, share)
+
+        def grad_group(g, d, pool_tile):
+            accs = []
             for t in range(4):
-                if g == 0:
-                    gacc[g, t] = new_acc(256)
-                else:
-                    gacc[g, t] = tps.tile([P, 256], F32, name="tbank")
-                grad_pass(gacc[g, t][:], g, t, 1, 0)
-        fin[1]()
-        fin = []
-        for g in range(2):
+                acc = pool_tile()
+                grad_pass(acc[:], g, t, d, 0)
+                grad_pass(acc[:], g, t, d, 1)
+                accs.append(acc)
+            return accs
+
+        def update_group(accs, g, d):
             for t in range(4):
-                grad_pass(gacc[g, t][:], g, t, 1, 1)
-                update(gacc[g, t][:], g, t, 1)
-            fin.append(planes(g, 1, 256 if g == 0 else 96))
-        fin[0]()
-        fin[1]()
+                update(accs[t][:], g, t, d)
+
+        def t_bank():
+            bank = tps.tile([P, 256], F32, name="tbank")
+            return bank
+
+        def a_bank():
+            return new_acc(256)
+
+        back1(3, [2])
+        q2 = back1_out(2)
+        a = grad_group(0, 0, t_bank)
+        back1(3, [3])
+        q3 = back1_out(3)
+        update_group(a, 0, 0)
+        q2()
+        f0 = planes(0, 0, 256)
+        a = grad_group(1, 0, t_bank)
+        update(a[0][:], 1, 0, 0)
+        update(a[1][:], 1, 1, 0)
+        q3()
+        update(a[2][:], 1, 2, 0)
+        update(a[3][:], 1, 3, 0)
+        f1 = planes(1, 0, 256)
+        f0()
+        update_group(grad_group(0, 1, a_bank), 0, 1)
+        f0 = planes(0, 1, 256)
+        f1()
+        update_group(grad_group(1, 1, t_bank), 1, 1)
+        f1 = planes(1, 1, 96)
+        f0()
+        f1()
+        for q4 in range(4):
+            queue = nc.sync if q4 % 2 else nc.scalar
+            queue.dma_start(
+                out=out_2[:, 4 * q4 : 4 * q4 + 4, :].bitcast(I32).rearrange("g r m -> r g m"),
+                in_=yq[1][32 * q4 : 32 * q4 + 4, :].bitcast(I32).rearrange("r (g m) -> r g m", g=2),
+            )

from contextlib import ExitStack

import concourse.mybir as mybir
from concourse.masks import make_identity

S, F, H, V, D = 1024, 1024, 1024, 4096, 512
FLOPS = 2 * S * F * H + 2 * S * V * D + 2 * S * H * D

F32 = mybir.dt.float32
BF16 = mybir.dt.bfloat16
U32 = mybir.dt.uint32
I32 = mybir.dt.int32
U8 = mybir.dt.uint8
FP8X4 = mybir.dt.float8_e4m3fn_x4
ALU = mybir.AluOpType
ACT = mybir.ActivationFunctionType

P = 128
PACK = 4
KP = P * PACK
A0 = 160
A1 = 192
S3 = 256
S5 = 512
S7 = 512
R0 = 0
PIECES = [(0, 256), (256, 256)]


def tile_output_bottleneck_update_h3_kernel(
    tc, prev, context, sample_weight, err, vocab, bottleneck, rate, out_0, out_1, out_2
):
    nc = tc.nc
    with ExitStack() as ctx:
        keep = ctx.enter_context(tc.tile_pool(name="keep", bufs=1))
        stage = ctx.enter_context(tc.tile_pool(name="stage", bufs=2))
        tps = ctx.enter_context(tc.psum_pool(name="tps", bufs=4))
        aps = ctx.enter_context(tc.psum_pool(name="aps", bufs=4))
        ctx.enter_context(tc.manual_schedule())

        def mx_tiles(pool, name, width, bufs=None):
            codes = pool.tile([P, width], U32, name=name + "_codes", bufs=bufs, align_bytes=64)
            scales = pool.tile([P, width], U8, name=name + "_scales", bufs=bufs, align_bytes=64)
            return codes, scales

        def load(name, shape, src, bufs):
            t = stage.tile(shape, BF16, name=name, bufs=bufs, align_bytes=64)
            nc.sync.dma_start(out=t[:], in_=src)
            return t

        def copy_on(engine, out, in_):
            if engine == "vector":
                nc.vector.tensor_copy(out=out, in_=in_)
            else:
                nc.scalar.copy(out=out, in_=in_)

        def interleave(engine, grouped, rows, c0, c1, run=4):
            copy_on(
                engine,
                grouped[:, c0:c1, :].rearrange("p (c i) t -> p c t i", i=run),
                rows[:, :, c0:c1].rearrange("p t (c i) -> p c t i", i=run),
            )

        def quantize(mx, c0, grouped_flat):
            n = grouped_flat.shape[1] // PACK
            nc.vector.quantize_mx(
                out=mx[0][:, c0 : c0 + n].bitcast(FP8X4), scales=mx[1][:, c0 : c0 + n], in_=grouped_flat
            )

        def mm(out, lhs, l0, rhs, r0, n, start, stop):
            nc.tensor.matmul_mx(
                out=out,
                lhsT=lhs[0][:, l0 : l0 + P].bitcast(FP8X4),
                lhsT_scale=lhs[1][:, l0 : l0 + P],
                rhs=rhs[0][:, r0 : r0 + n].bitcast(FP8X4),
                rhs_scale=rhs[1][:, r0 : r0 + n],
                start=start,
                stop=stop,
            )

        def transpose_unit(rows, ready):
            words = rows.bitcast(F32)
            bank = tps.tile([P, 2, 2, P], F32, name="tbank")
            for g in range(2):
                for u in range(2):
                    src = words[:, 256 * g + P * u : 256 * g + P * (u + 1)] if ready else words[:, 256 * g + u : 256 * (g + 1) : 2]
                    nc.tensor.transpose(bank[:, g, u, :], src, ident[:])
            return bank

        def empty_unit(engine, bank, grouped, j):
            dst = grouped[:, 1024 * j : 1024 * (j + 1)].bitcast(F32).rearrange("p (g r u) -> p g r u", g=2, u=2)
            copy_on(engine, dst, bank[:].rearrange("p g u r -> p g r u"))

        def turn(sources, engines, ready=False):
            halves = []
            for h in range(2):
                grouped = stage.tile([P, 2048], BF16, name="turned", bufs=4, align_bytes=64)
                for j in range(2):
                    bank = transpose_unit(sources[2 * h + j], ready)
                    empty_unit(engines[2 * h + j], bank, grouped, j)
                halves.append(grouped)
            return halves

        def quantize_turned(halves):
            res = []
            for h in range(2):
                mx = mx_tiles(stage, "tq", 512, 10)
                quantize(mx, 0, halves[h][:])
                res.append(mx)
            return res

        ident = keep.tile([P, P], F32, name="ident")
        make_identity(nc, ident[:])
        warm = keep.tile([P, 1], F32, name="warm")
        nc.scalar.activation(out=warm[:], in_=ident[:, 0:1], func=ACT.Tanh)

        def slots(x, g):
            return x[KP * g : KP * (g + 1), :].rearrange("(p t) c -> p t c", t=PACK)

        def load_k(src):
            return load("krows", [P, PACK, 512], src, 7)

        def load_s(shape, src):
            return load("srows", shape, src, 4)

        def flat(grouped):
            return grouped[:].rearrange("p c t -> p (c t)")

        def new_grouped(width=512):
            grouped = stage.tile([P, width, PACK], BF16, name="grouped", bufs=4, align_bytes=64)
            return grouped

        vq = [mx_tiles(keep, "vq%d" % k, D) for k in range(8)]
        cq = [[mx_tiles(keep, "cq%d%d" % (k, g), 512) for g in range(2)] for k in range(2)]
        hq = [[mx_tiles(keep, "hq%d%d" % (s, g), 512) for g in range(2)] for s in range(2)]
        bq0 = mx_tiles(keep, "bq0", D)
        bq1 = [mx_tiles(keep, "bq1%d" % d0, w) for d0, w in PIECES]
        SC4 = ["scalar"] * 4

        def regroup(src, mx, share):
            width = src.shape[2]
            grouped = new_grouped(width)
            if share:
                interleave("scalar", grouped, src, 0, share)
            if share < width:
                interleave("vector", grouped, src, share, width)
            return lambda: quantize(mx, 0, flat(grouped))

        def pre_pass(accs, pq, k, g):
            for t in range(4):
                mm(accs[t][:], pq[t // 2], 256 * (t % 2) + P * k, cq[k][g], 0, 512, k == 0, k == 1)

        def tanh_out(th, t, acc):
            nc.scalar.activation(
                out=th[:, t, :].rearrange("p (j m) -> p j m", j=PACK),
                in_=acc[:].rearrange("p (m j) -> p j m", j=PACK),
                func=ACT.Tanh,
            )

        def new_th():
            th = stage.tile([P, PACK, 512], F32, name="th", bufs=4, align_bytes=64)
            return th

        def new_acc(n=512):
            acc = aps.tile([P, n], F32, name="acc")
            return acc

        def pre_block(g, pq):
            th = new_th()
            for t in range(4):
                acc = new_acc()
                for k in range(2):
                    mm(acc[:], pq[t // 2], 256 * (t % 2) + P * k, cq[k][g], 0, 512, k == 0, k == 1)
                tanh_out(th, t, acc)
            return th

        def weigh(s, g, th):
            grouped = new_grouped()
            nc.vector.tensor_tensor(
                out=grouped[:].rearrange("p (c i) t -> p c t i", i=2),
                in0=th[:].rearrange("p t (c i) -> p c t i", i=2),
                in1=w32[:, s, :].unsqueeze(1).unsqueeze(3).to_broadcast([P, 256, PACK, 2]),
                op=ALU.mult,
            )
            return lambda: quantize(hq[s][g], 0, flat(grouped))

        craw = {}
        e0, vraw, e1, braw = {}, {}, {}, {}

        def load_c(k, g):
            craw[k, g] = load_k(slots(context, k)[:, :, 512 * g : 512 * (g + 1)])

        def load_v(k):
            vraw[k] = load_k(slots(vocab, k))

        def load_e0(c):
            e0[c] = load_s([P, PACK, 1024], slots(err, 0)[:, :, 1024 * c : 1024 * (c + 1)])

        def load_e1(t):
            e1[t] = load_s([P, V], slots(err, 1)[:, t, :])

        def turn_e0(c):
            return turn([e0[c][:, t, :] for t in range(4)], SC4)

        def turn_e1(t):
            return turn([e1[t][:, 1024 * j : 1024 * (j + 1)] for j in range(4)], SC4)

        p0 = [load("p0", [P, F], slots(prev, 0)[:, t, :], 4) for t in range(4)]
        load_c(0, 0)
        p1 = load_s([P, PACK, F], slots(prev, 1))
        load_c(1, 0)
        load_e0(0)
        load_c(0, 1)
        load_c(1, 1)
        load_e0(1)
        load_v(0)
        load_v(1)
        load_v(2)
        w_raw = load("w_raw", [P, 2, PACK], sample_weight.rearrange("(g p t) -> p g t", g=2, t=PACK), 1)
        r_raw = load("r_raw", [P, 2, PACK], rate.rearrange("(g p t) -> p g t", g=2, t=PACK), 1)

        hp = turn([p0[t][:] for t in range(4)], SC4)
        pq0 = [mx_tiles(stage, "tq", 512, 10) for h in range(2)]
        quantize(pq0[0], 0, hp[0][:])
        q0 = regroup(craw[0, 0], cq[0][0], A0)
        quantize(pq0[1], 0, hp[1][:])
        q0()
        load_v(3)
        accs = [new_acc() for t in range(4)]
        pre_pass(accs, pq0, 0, 0)
        regroup(craw[1, 0], cq[1][0], A1)()
        hp = turn([p1[:, t, :] for t in range(4)], ["scalar", "vector", "vector", "vector"])
        load_e0(2)
        load_v(4)
        pre_pass(accs, pq0, 1, 0)
        th = {}
        th[0, 0] = new_th()
        for t in range(4):
            tanh_out(th[0, 0], t, accs[t])
        pq1 = quantize_turned(hp)
        halves = turn_e0(0)
        q0 = regroup(craw[0, 1], cq[0][1], 0)
        q1 = regroup(craw[1, 1], cq[1][1], 0)
        q0()
        q1()
        eq = {0: quantize_turned(halves)}
        load_v(5)
        load_e0(3)
        load_v(6)
        th[1, 0] = pre_block(0, pq1)
        halves = turn_e0(1)
        qa = regroup(vraw[0], vq[0], 0)
        qb = regroup(vraw[1], vq[1], 0)
        qa()
        qb()
        eq[1] = quantize_turned(halves)
        load_v(7)
        load_e1(0)
        th[0, 1] = pre_block(1, pq0)
        th[1, 1] = pre_block(1, pq1)
        w32 = keep.tile([P, 2, PACK], F32, name="w32")
        neg_rate = keep.tile([P, 2, PACK], F32, name="neg_rate")

        acc0 = [new_acc() for t in range(4)]

        def back0_passes(c):
            for t in range(4):
                for g in range(2):
                    mm(acc0[t][:], eq[c][t // 2], 256 * (t % 2) + P * g, vq[2 * c + g], 0, D, c == 0 and g == 0, c == 3 and g == 1)

        fq = {}
        qa = regroup(vraw[2], vq[2], 0)
        qb = regroup(vraw[3], vq[3], S3)
        nc.vector.tensor_copy(out=w32[:], in_=w_raw[:])
        nc.vector.tensor_scalar(out=neg_rate[:], in0=r_raw[:], scalar1=-1.0, scalar2=None, op0=ALU.mult)
        qa()
        back0_passes(0)
        halves = turn_e0(2)
        load_e1(1)
        qa = regroup(vraw[4], vq[4], 0)
        qb()
        qa()
        qb = regroup(vraw[5], vq[5], S5)
        eq[2] = quantize_turned(halves)
        back0_passes(1)
        halves = turn_e0(3)
        load_e1(2)
        qa = regroup(vraw[6], vq[6], 0)
        qb()
        qa()
        qb = regroup(vraw[7], vq[7], S7)
        qh = weigh(0, 0, th[0, 0])
        eq[3] = quantize_turned(halves)
        qb()
        qh()
        back0_passes(2)
        halves = turn_e1(0)
        load_e1(3)
        for g in range(2):
            braw[g] = load_k(slots(bottleneck, g))
        qh = weigh(1, 0, th[1, 0])
        fq[0] = quantize_turned(halves)
        qh()
        back0_passes(3)
        rows0 = stage.tile([P, PACK, D], BF16, name="rows0", bufs=1, align_bytes=64)
        for t in range(0, 2):
            nc.scalar.copy(out=rows0[:, t, :], in_=acc0[t][:])
        halves = turn_e1(1)
        for t in range(2, 4):
            nc.scalar.copy(out=rows0[:, t, :], in_=acc0[t][:])
        qh = weigh(0, 1, th[0, 1])
        fq[1] = quantize_turned(halves)
        qh()
        acc1 = [aps.tile([P, PACK, P], F32, name="acc") for j in range(4)]

        def back1(t, quarters):
            for j in quarters:
                for k in range(8):
                    mm(acc1[j][:, t, :], fq[t][k // 4], P * (k % 4), vq[k], P * j, P, k == 0, k == 7)

        def back1_out(j):
            grouped = new_grouped(P)
            nc.scalar.copy(out=grouped[:], in_=acc1[j][:].rearrange("p t d -> p d t"))
            return lambda: quantize(bq1[j // 2], P * (j % 2), flat(grouped))

        back1(0, [0, 1])
        halves = turn_e1(2)
        qh = weigh(1, 1, th[1, 1])
        fq[2] = quantize_turned(halves)
        qh()
        back1(0, [2, 3])
        back1(1, [0, 1])
        halves = turn_e1(3)
        qb = regroup(rows0, bq0, R0)
        fq[3] = quantize_turned(halves)
        qb()
        back1(2, [0, 1])
        back1(1, [2, 3])
        for j in range(2):
            back1(3, [j])
            back1_out(j)()
        back1(2, [2, 3])

        ys = {}
        yq = mx_tiles(keep, "yq", 2 * D)

        def grad_pass(acc, g, t, d, s):
            d0, w = PIECES[d]
            if s == 0:
                mm(acc, hq[0][g], P * t, bq0, d0, w, True, False)
            else:
                mm(acc, hq[1][g], P * t, bq1[d], 0, w, False, True)

        def update(acc, g, t, d):
            d0, w = PIECES[d]
            if t == 0:
                ys[d, g] = new_th()
            y = ys[d, g]
            nc.vector.scalar_tensor_tensor(
                out=y[:, t, 0:w], in0=acc, scalar=neg_rate[:, g, t : t + 1], in1=braw[g][:, t, d0 : d0 + w],
                op0=ALU.mult, op1=ALU.add,
            )
            if t % 2:
                nc.sync.dma_start(out=slots(out_0, g)[:, t - 1 : t + 1, d0 : d0 + w], in_=y[:, t - 1 : t + 1, 0:w])

        def planes(g, d, share):
            d0, w = PIECES[d]
            grouped = new_grouped(w)
            interleave("scalar", grouped, ys[d, g], 0, share, 2)
            if share < w:
                interleave("vector", grouped, ys[d, g], share, w, 2)

            def finish():
                quantize(yq, D * g + d0, flat(grouped))
                cols = slice(d0, d0 + w)
                nc.sync.dma_start(
                    out=out_1[g, :, cols, :].rearrange("p m t -> p (m t)").bitcast(I32), in_=yq[0][:, D * g + d0 : D * g + d0 + w].bitcast(I32)
                )

            return finish

        def grad_closed(g, d, share):
            d0, w = PIECES[d]
            for tp in range(2):
                bank = tps.tile([P, 2, w], F32, name="tbank")
                for i in range(2):
                    grad_pass(bank[:, i, :], g, 2 * tp + i, d, 0)
                    grad_pass(bank[:, i, :], g, 2 * tp + i, d, 1)
                for i in range(2):
                    update(bank[:, i, :], g, 2 * tp + i, d)
            return planes(g, d, share)

        def grad_group(g, d, pool_tile):
            accs = []
            for t in range(4):
                acc = pool_tile()
                grad_pass(acc[:], g, t, d, 0)
                grad_pass(acc[:], g, t, d, 1)
                accs.append(acc)
            return accs

        def update_group(accs, g, d):
            for t in range(4):
                update(accs[t][:], g, t, d)

        def t_bank():
            bank = tps.tile([P, 256], F32, name="tbank")
            return bank

        def a_bank():
            return new_acc(256)

        back1(3, [2])
        q2 = back1_out(2)
        a = grad_group(0, 0, t_bank)
        back1(3, [3])
        q3 = back1_out(3)
        update_group(a, 0, 0)
        q2()
        f0 = planes(0, 0, 256)
        a = grad_group(1, 0, t_bank)
        update(a[0][:], 1, 0, 0)
        update(a[1][:], 1, 1, 0)
        q3()
        update(a[2][:], 1, 2, 0)
        update(a[3][:], 1, 3, 0)
        f1 = planes(1, 0, 256)
        f0()
        update_group(grad_group(0, 1, a_bank), 0, 1)
        f0 = planes(0, 1, 256)
        f1()
        update_group(grad_group(1, 1, t_bank), 1, 1)
        f1 = planes(1, 1, 96)
        f0()
        f1()
        for q4 in range(4):
            queue = nc.sync if q4 % 2 else nc.scalar
            queue.dma_start(
                out=out_2[:, 4 * q4 : 4 * q4 + 4, :].bitcast(I32).rearrange("g r m -> r g m"),
                in_=yq[1][32 * q4 : 32 * q4 + 4, :].bitcast(I32).rearrange("r (g m) -> r g m", g=2),
            )
